import numpy as np
CORES = [3,11,19,27,35,43,51,59,67,75,83,91,99,107,115,123]
N = 16
H = 4
PERIODIC = True
def setup_inputs(rng):
    return {"x": rng.standard_normal((N, 128, 64), dtype=np.float32)}
def reference(x):
    W = x.shape[2]
    y = np.zeros((N, 128, W + 2 * H), x.dtype)
    for r in range(N):
        y[r][:, H:H + W] = x[r]
        left, right = r - 1, r + 1
        if PERIODIC:
            left, right = left % N, right % N
        if 0 <= left < N:
            y[r][:, :H] = x[left][:, W - H:]
        if 0 <= right < N:
            y[r][:, W + H:] = x[right][:, :H]
    return {"y": y}

@@ -1,0 +1,49 @@
+import concourse.bass as bass
+
+H = 4
+W = 64
+
+SCRATCH = {
+    "buf": ("sbuf", [128, W + 2 * H], "float32"),
+}
+SEMAPHORES = ["local", "arrived"]
+
+
+def rank_program(g, core, T, topo):
+    rank = T.rank_of(core)
+    if rank is None:
+        return
+    n = len(T.cores)
+    left = T.cores[(rank - 1) % n]
+    right = T.cores[(rank + 1) % n]
+    buf = T.buf
+
+    g.dma_start(out=buf[:, H:H + W], in_=T.x[:, :]).then_inc(T.sem.local, 16)
+    g.wait_ge(T.sem.local, 16)
+
+    l_rid, l_pid = topo.addr(left)[:2]
+    r_rid, r_pid = topo.addr(right)[:2]
+    g.remote_dma_fused(
+        [
+            bass.RemoteDMATransfer(
+                dst_ids=[bass.DstId(rid=l_rid, pnc=l_pid)],
+                dma_engine_mask=0x0F,
+                remote_sem=T.sem.arrived,
+                src=buf[:, H:2 * H],
+                dst=buf[:, H + W:H + W + H],
+            ),
+            bass.RemoteDMATransfer(
+                dst_ids=[bass.DstId(rid=r_rid, pnc=r_pid)],
+                dma_engine_mask=0xF0,
+                remote_sem=T.sem.arrived,
+                src=buf[:, W:H + W],
+                dst=buf[:, 0:H],
+            ),
+        ],
+        local_sem=T.sem.arrived,
+    )
+
+    g.wait_ge(T.sem.arrived, 16)
+
+    g.dma_start(out=T.y[:, :], in_=buf[:, :]).then_inc(T.sem.local, 16)
+    g.wait_ge(T.sem.local, 32)

@@ -1,5 +1,3 @@
-import concourse.bass as bass
-
 H = 4
 W = 64
 
@@ -21,29 +19,17 @@ def rank_program(g, core, T, topo):
     g.dma_start(out=buf[:, H:H + W], in_=T.x[:, :]).then_inc(T.sem.local, 16)
     g.wait_ge(T.sem.local, 16)
 
-    l_rid, l_pid = topo.addr(left)[:2]
-    r_rid, r_pid = topo.addr(right)[:2]
-    g.remote_dma_fused(
-        [
-            bass.RemoteDMATransfer(
-                dst_ids=[bass.DstId(rid=l_rid, pnc=l_pid)],
-                dma_engine_mask=0x0F,
-                remote_sem=T.sem.arrived,
-                src=buf[:, H:2 * H],
-                dst=buf[:, H + W:H + W + H],
-            ),
-            bass.RemoteDMATransfer(
-                dst_ids=[bass.DstId(rid=r_rid, pnc=r_pid)],
-                dma_engine_mask=0xF0,
-                remote_sem=T.sem.arrived,
-                src=buf[:, W:H + W],
-                dst=buf[:, 0:H],
-            ),
-        ],
-        local_sem=T.sem.arrived,
-    )
+    sends = [
+        (left, buf[:, H:2 * H], buf[:, H + W:H + W + H]),
+        (right, buf[:, W:H + W], buf[:, 0:H]),
+    ]
+    sends.sort(key=lambda s: 1 if topo.mates(topo.chip(core), topo.chip(s[0])) else 0)
+    for dst_core, src, dst in sends:
+        rid, pid = topo.addr(dst_core)[:2]
+        g.remote_dma(out_ap=dst, in_ap=src, remote_sem=T.sem.arrived, local_sem=T.sem.arrived,
+                     pid=pid, routing_id=rid, dma_engine_mask=topo.mask(core, dst_core))
 
-    g.wait_ge(T.sem.arrived, 16)
+    g.wait_ge(T.sem.arrived, 32)
 
     g.dma_start(out=T.y[:, :], in_=buf[:, :]).then_inc(T.sem.local, 16)
     g.wait_ge(T.sem.local, 32)

H = 4
W = 64

SCRATCH = {
    "buf": ("sbuf", [128, W + 2 * H], "float32"),
}
SEMAPHORES = ["local", "arrived"]


def rank_program(g, core, T, topo):
    rank = T.rank_of(core)
    if rank is None:
        return
    n = len(T.cores)
    left = T.cores[(rank - 1) % n]
    right = T.cores[(rank + 1) % n]
    buf = T.buf

    g.dma_start(out=buf[:, H:H + W], in_=T.x[:, :]).then_inc(T.sem.local, 16)
    g.wait_ge(T.sem.local, 16)

    sends = [
        (left, buf[:, H:2 * H], buf[:, H + W:H + W + H]),
        (right, buf[:, W:H + W], buf[:, 0:H]),
    ]
    sends.sort(key=lambda s: 1 if topo.mates(topo.chip(core), topo.chip(s[0])) else 0)
    for dst_core, src, dst in sends:
        rid, pid = topo.addr(dst_core)[:2]
        g.remote_dma(out_ap=dst, in_ap=src, remote_sem=T.sem.arrived, local_sem=T.sem.arrived,
                     pid=pid, routing_id=rid, dma_engine_mask=topo.mask(core, dst_core))

    g.wait_ge(T.sem.arrived, 32)

    g.dma_start(out=T.y[:, :], in_=buf[:, :]).then_inc(T.sem.local, 16)
    g.wait_ge(T.sem.local, 32)
